import numpy as np
import ml_dtypes


def mxq(x, axis, fmt="e4m3"):
    dtype, down = {"e4m3": (ml_dtypes.float8_e4m3fn, 7), "e5m2": (ml_dtypes.float8_e5m2, 14)}[fmt]
    v = np.moveaxis(np.asarray(x, np.float32).astype(ml_dtypes.bfloat16).astype(np.float64), axis, -1)
    blocks = v.reshape(v.shape[:-1] + (-1, 32))
    amax = np.abs(blocks).max(-1, keepdims=True)
    byte = np.maximum(np.where(amax > 0, np.frexp(amax)[1] - 1 + 127, 0) - down, 1)
    scale = np.exp2(byte - 127.0)
    codes = (blocks / scale).astype(np.float32).astype(dtype).astype(np.float64)
    return np.moveaxis((codes * scale).reshape(v.shape), -1, axis)


WIDE = False


def mx_kscale(k):
    if not WIDE:
        return np.ones(k)
    levels = np.array([30, -30])
    if k % 512:
        return np.exp2(np.random.permutation(np.resize(levels, k // 32))).repeat(32)
    a = np.empty((k // 512, 16))
    for p in range(k // 512):
        a[p, :8] = np.random.permutation(np.resize(levels, 8))
        for g in range(8):
            far = levels[np.abs(levels - a[p, g]) >= 10]
            a[p, g + 8] = far[np.random.randint(len(far))]
    return np.exp2(a.ravel()).repeat(32)


def f64(x):
    return np.asarray(x).astype(np.float64)


def striped(idx):
    return np.tile(np.asarray(idx).reshape(-1, 16).T, (8, 1)).astype(np.uint16)


def unstriped(offs):
    return offs[:16].T.reshape(-1).astype(np.int64)


E2M1 = np.array([0.0, 0.5, 1.0, 1.5, 2.0, 3.0, 4.0, 6.0, -0.0, -0.5, -1.0, -1.5, -2.0, -3.0, -4.0, -6.0])


def pack_weight(w, fmt):
    k, n = w.shape
    w = f64(np.asarray(w, np.float32).astype(ml_dtypes.bfloat16)).reshape(k // 32, 32, n)
    amax = np.abs(w).max(1)
    if fmt in ("e4m3", "e5m2"):
        byte = np.frexp(amax)[1] - 1 + 127 - (7 if fmt == "e4m3" else 14)
    else:
        mant, ex = np.frexp(amax / 6.0)
        byte = np.where(mant > 0.5, ex, ex - 1) + 127
    byte = np.clip(np.where(amax > 0, byte, 1), 1, 254)
    scaled = (w * np.exp2(127.0 - byte)[:, None, :]).reshape(k, n).astype(np.float32)
    by_word = np.ascontiguousarray(scaled.reshape(k // 512, 128, 4, n).transpose(0, 1, 3, 2))
    if fmt in ("e4m3", "e5m2"):
        words = by_word.astype(ml_dtypes.float8_e4m3fn if fmt == "e4m3" else ml_dtypes.float8_e5m2).view(np.uint8)
    else:
        c = by_word.astype(ml_dtypes.float4_e2m1fn).view(np.uint8) & 0xF
        words = (c[..., 0::2] | (c[..., 1::2] << 4)).reshape(k // 512, 128, 2 * n)
    return np.ascontiguousarray(words), np.ascontiguousarray(byte.astype(np.uint8).reshape(k // 512, 16, n))


def unpack_weight(words, scales, fmt):
    g, _, n = scales.shape
    words = np.ascontiguousarray(words).reshape(g, 128, n, -1)
    if fmt in ("e4m3", "e5m2"):
        vals = words.view(ml_dtypes.float8_e4m3fn if fmt == "e4m3" else ml_dtypes.float8_e5m2).astype(np.float64)
    else:
        nib = np.empty((g, 128, n, 4), np.uint8)
        nib[..., 0::2] = words & 0xF
        nib[..., 1::2] = words >> 4
        vals = E2M1[nib]
    vals = vals * np.repeat(np.exp2(scales.astype(np.float64) - 127.0), 8, axis=1)[..., None]
    return vals.transpose(0, 1, 3, 2).reshape(g * 512, n)


K, T, J, R, F, Z, X, O, N, S, E = 512, 1024, 256, 512, 512, 1024, 1024, 128, 256, 1024, 1024


def setup_inputs():
    n = np.random.standard_normal
    idx = np.random.permutation(T)[:J]
    idx2 = np.random.permutation(Z)[:J]
    idx3 = np.random.permutation(J)[:O]
    idx4 = np.random.permutation(X)[:O]
    idx5 = np.random.permutation(X)[:O]
    idx6 = np.random.permutation(S)[:N]
    idx7 = np.random.permutation(E)[:O]
    fk = mx_kscale(K)
    ff = mx_kscale(F)
    fr = mx_kscale(R)
    xtp = pack_weight(n((K, T)) / fk[:, None], "e4m3")
    xop = pack_weight(n((F, Z)) / ff[:, None], "e2m1")
    wp = pack_weight(n((K, R)) * 1 / np.sqrt(K) * fk[:, None] * fr, "e2m1")
    w0p = pack_weight(n((F, R)) * 1 / np.sqrt(F) * ff[:, None] * fr, "e5m2")
    vsp = pack_weight(n((R, S)) * 1 / np.sqrt(R) / fr[:, None], "e5m2")
    return {
        "xt_words": xtp[0],
        "xt_scales": xtp[1],
        "xo_words": xop[0],
        "xo_scales": xop[1],
        "w_words": wp[0],
        "w_scales": wp[1],
        "w0_words": w0p[0],
        "w0_scales": w0p[1],
        "tb": (n((R, X)) * 1.0).astype(np.float32),
        "vs_words": vsp[0],
        "vs_scales": vsp[1],
        "offs": striped(idx),
        "offs2": striped(idx2),
        "offs3": striped(idx3),
        "offs4": striped(idx4),
        "offs5": striped(idx5),
        "offs6": striped(idx6),
        "offs7": striped(idx7),
    }


def reference(xt_words, xt_scales, xo_words, xo_scales, w_words, w_scales, w0_words, w0_scales, tb, vs_words, vs_scales, offs, offs2, offs3, offs4, offs5, offs6, offs7):
    idx = unstriped(offs)
    idx2 = unstriped(offs2)
    idx3 = unstriped(offs3)
    idx4 = unstriped(offs4)
    idx5 = unstriped(offs5)
    idx6 = unstriped(offs6)
    idx7 = unstriped(offs7)
    xtu = unpack_weight(xt_words, xt_scales, "e4m3")
    xou = unpack_weight(xo_words, xo_scales, "e2m1")
    wu = unpack_weight(w_words, w_scales, "e2m1")
    w0u = unpack_weight(w0_words, w0_scales, "e5m2")
    vsu = unpack_weight(vs_words, vs_scales, "e5m2")
    xtidxg = xtu[:, idx]
    xoidx2g = xou[:, idx2]
    a = wu.T @ xtidxg + w0u.T @ xoidx2g
    la = a[:, 0:1]
    la2 = a[:, 128:129]
    hid = np.maximum(np.minimum(a[:, idx3], f64(tb)[:, idx4] * la), f64(tb)[:, idx5] * la2)
    vsidx6g = vsu[:, idx6]
    hidq = mxq(hid, 0, "e4m3")
    p = vsidx6g.T @ hidq
    y = np.zeros((N, E))
    y[:, idx7] = p
    return y

@@ -1,0 +1,177 @@
+from contextlib import ExitStack
+
+import concourse.mybir as mybir
+
+F32 = mybir.dt.float32
+BF16 = mybir.dt.bfloat16
+I32 = mybir.dt.int32
+U32 = mybir.dt.uint32
+U16 = mybir.dt.uint16
+U8 = mybir.dt.uint8
+E4M3 = mybir.dt.float8_e4m3fn_x4
+E5M2 = mybir.dt.float8_e5m2_x4
+E2M1 = mybir.dt.float4_e2m1fn_x4
+COPY = mybir.ActivationFunctionType.Copy
+MIN = mybir.AluOpType.min
+MAX = mybir.AluOpType.max
+
+P = 128
+PACK = 4
+QUADS = 4
+QUAD = 32
+T, J, R, X, O, N, E = 1024, 256, 512, 1024, 128, 256, 1024
+
+FLOPS = 2 * 512 * (2 * R * J + N * O)
+
+
+def tile_list_leadbounds_bank_store_scattered_kernel(
+    tc, xt_words, xt_scales, xo_words, xo_scales, w_words, w_scales, w0_words, w0_scales, tb,
+    vs_words, vs_scales, offs, offs2, offs3, offs4, offs5, offs6, offs7, out,
+):
+    nc = tc.nc
+    with ExitStack() as ctx:
+        lists = ctx.enter_context(tc.tile_pool(name="lists", bufs=1))
+        sb = ctx.enter_context(tc.tile_pool(name="sb", bufs=1))
+        ps = ctx.enter_context(tc.psum_pool(name="ps", bufs=1))
+
+        def load_list(name, src):
+            tile = lists.tile(list(src.shape), U16, name=name)
+            nc.sync.dma_start(tile[:], src)
+            return tile
+
+        def load_words(queue, name, src, columns, dtype):
+            tile = sb.tile([P, columns], dtype, name=name, align_bytes=64)
+            queue.dma_start(out=tile[:].bitcast(I32), in_=src.bitcast(I32))
+            return tile
+
+        def load_scales(engine, queue, name, src):
+            tile = sb.tile([P, T], U8, name=name, align_bytes=64)
+            engine.memset(tile[:].bitcast(I32), 0)
+            for q in range(QUADS):
+                queue.dma_start(
+                    out=tile[QUAD * q : QUAD * q + 4, :].bitcast(I32),
+                    in_=src[0, 4 * q : 4 * q + 4, :].bitcast(I32),
+                )
+            return tile
+
+        def gather(name, window, offsets, count, dtype):
+            tile = sb.tile([P, count], dtype, name=name, align_bytes=64)
+            nc.vector.tensor_copy(out=tile[:], in_=window[:].indirect(offsets[:]))
+            return tile
+
+        flat = lambda words: words[0].rearrange("p c t -> p (c t)")
+
+        xt_w = load_words(nc.scalar, "xt_w", flat(xt_words), T, U32)
+        ws_rows = sb.tile([4, QUADS, 2, R], U8, name="ws_rows", align_bytes=64)
+        for i, src in enumerate((w_scales, w0_scales)):
+            nc.sync.dma_start(
+                out=ws_rows[:, :, i, :].bitcast(I32),
+                in_=src[0].rearrange("(q r) c -> r q c", r=4).bitcast(I32),
+            )
+        l1 = load_list("l1", offs)
+        xt_s = load_scales(nc.vector, nc.sync, "xt_s", xt_scales)
+        w_w = load_words(nc.sync, "w_w", w_words[0], R, U16)
+        w0_w = load_words(nc.sync, "w0_w", flat(w0_words), R, U32)
+        l2 = load_list("l2", offs2)
+        xo_s = load_scales(nc.vector, nc.sync, "xo_s", xo_scales)
+        xo_w = load_words(nc.sync, "xo_w", xo_words[0], T, U16)
+        vs_s = load_scales(nc.gpsimd, nc.gpsimd, "vs_s", vs_scales)
+
+        tb_rows = tb.rearrange("(p t) x -> t p x", t=PACK)
+        tb_t = [sb.tile([P, X], F32, name="tb%d" % t) for t in range(PACK)]
+        nc.sync.dma_start(out=tb_t[0][:], in_=tb_rows[0])
+        l4 = load_list("l4", offs4)
+        l5 = load_list("l5", offs5)
+        l3 = load_list("l3", offs3)
+        l6 = load_list("l6", offs6)
+        for t in range(1, PACK):
+            nc.sync.dma_start(out=tb_t[t][:], in_=tb_rows[t])
+        vs_w = load_words(nc.sync, "vs_w", flat(vs_words), T, U32)
+        l7 = load_list("l7", offs7)
+
+        pages = [sb.tile([P, E], F32, name="page%d" % h) for h in range(2)]
+        for page in pages:
+            nc.vector.memset(page[:], 0.0)
+
+        ws_plane = sb.tile([P, 2 * R], U8, name="ws_plane", align_bytes=64)
+        nc.vector.memset(ws_plane[:].bitcast(I32), 0)
+        for q in range(QUADS):
+            nc.vector.tensor_copy(
+                out=ws_plane[QUAD * q : QUAD * q + 4, :].bitcast(I32),
+                in_=ws_rows[:, q, :, :].rearrange("r i c -> r (i c)").bitcast(I32),
+            )
+        ws_d = sb.tile([P, 2, PACK, P], U8, name="ws_d", align_bytes=64)
+        nc.vector.tensor_copy(
+            out=ws_d[:].rearrange("p i t m -> p i m t"),
+            in_=ws_plane[:].rearrange("p (i m t) -> p i m t", i=2, t=PACK),
+        )
+        w_d = sb.tile([P, PACK, P], U16, name="w_d", align_bytes=64)
+        w0_d = sb.tile([P, PACK, P], U32, name="w0_d", align_bytes=64)
+        for dealt, raw in ((w_d, w_w), (w0_d, w0_w)):
+            nc.scalar.copy(
+                out=dealt[:].rearrange("p t m -> p m t"),
+                in_=raw[:].rearrange("p (m t) -> p m t", t=PACK),
+            )
+
+        xt_sg = gather("xt_sg", xt_s, l1, J, U8)
+        xt_g = gather("xt_g", xt_w, l1, J, U32)
+        xo_sg = gather("xo_sg", xo_s, l2, J, U8)
+        xo_g = gather("xo_g", xo_w, l2, J, U16)
+
+        acc = [ps.tile([P, J], F32, name="acc%d" % t) for t in range(PACK)]
+        for t in range(PACK):
+            nc.tensor.matmul_mx(
+                out=acc[t][:], lhsT=w_d[:, t, :].bitcast(E2M1), lhsT_scale=ws_d[:, 0, t, :],
+                rhs=xt_g[:].bitcast(E4M3), rhs_scale=xt_sg[:], start=True, stop=False,
+            )
+        for t in range(PACK):
+            nc.tensor.matmul_mx(
+                out=acc[t][:], lhsT=w0_d[:, t, :].bitcast(E5M2), lhsT_scale=ws_d[:, 1, t, :],
+                rhs=xo_g[:].bitcast(E2M1), rhs_scale=xo_sg[:], start=False, stop=True,
+            )
+
+        vs_sg = gather("vs_sg", vs_s, l6, N, U8)
+
+        picked = sb.tile([P, PACK, O], F32, name="picked")
+        upper = sb.tile([P, PACK, O], F32, name="upper")
+        lower = sb.tile([P, PACK, O], F32, name="lower")
+        cut = sb.tile([P, PACK, O], F32, name="cut")
+        for t in range(PACK):
+            a_t = sb.tile([P, J], F32, name="a%d" % t)
+            if t < 2:
+                nc.vector.tensor_copy(out=a_t[:], in_=acc[t][:])
+            else:
+                nc.scalar.copy(out=a_t[:], in_=acc[t][:])
+            nc.scalar.activation(out=upper[:, t, :], in_=tb_t[t][:].indirect(l4[:]), func=COPY, scale=a_t[:, 0:1])
+            nc.scalar.activation(out=lower[:, t, :], in_=tb_t[t][:].indirect(l5[:]), func=COPY, scale=a_t[:, 128:129])
+            nc.vector.tensor_copy(out=picked[:, t, :], in_=a_t[:].indirect(l3[:]))
+            nc.vector.tensor_tensor(out=cut[:, t, :], in0=picked[:, t, :], in1=upper[:, t, :], op=MIN)
+
+        hid = sb.tile([P, O * PACK], BF16, name="hid", align_bytes=64)
+        nc.vector.tensor_tensor(
+            out=hid[:].rearrange("p (c i t) -> p c t i", i=4, t=PACK),
+            in0=cut[:].rearrange("p t (c i) -> p c t i", i=4),
+            in1=lower[:].rearrange("p t (c i) -> p c t i", i=4),
+            op=MAX,
+        )
+        vs_g = gather("vs_g", vs_w, l6, N, U32)
+        hid_w = sb.tile([P, O], U32, name="hid_w", align_bytes=64)
+        hid_s = sb.tile([P, O], U8, name="hid_s", align_bytes=64)
+        nc.vector.quantize_mx(out=hid_w[:].bitcast(E4M3), scales=hid_s[:], in_=hid[:])
+
+        for h in range(2):
+            cols = slice(P * h, P * (h + 1))
+            prod = ps.tile([P, O], F32, name="prod%d" % h)
+            nc.tensor.matmul_mx(
+                out=prod[:], lhsT=vs_g[:, cols].bitcast(E5M2), lhsT_scale=vs_sg[:, cols],
+                rhs=hid_w[:].bitcast(E4M3), rhs_scale=hid_s[:], start=True, stop=True,
+            )
+            p_h = sb.tile([P, O], F32, name="p%d" % h)
+            if h == 0:
+                nc.vector.tensor_copy(out=p_h[:], in_=prod[:])
+                nc.vector.tensor_copy(out=pages[h][:].indirect(l7[:]), in_=p_h[:])
+                nc.sync.dma_start(out=out[cols, :], in_=pages[h][:])
+            else:
+                nc.scalar.copy(out=p_h[:], in_=prod[:])
+                nc.scalar.activation(out=pages[h][:].indirect(l7[:]), in_=p_h[:], func=COPY)
+                nc.scalar.dma_start(out=out[cols, :], in_=pages[h][:])

@@ -61,50 +61,55 @@ def tile_list_leadbounds_bank_store_scattered_kernel(
 
         flat = lambda words: words[0].rearrange("p c t -> p (c t)")
 
-        xt_w = load_words(nc.scalar, "xt_w", flat(xt_words), T, U32)
+        def load_rows(queue, rows, src):
+            queue.dma_start(out=rows.bitcast(I32), in_=src[0].rearrange("(q r) c -> r q c", r=4).bitcast(I32))
+
+        def spread(name, rows):
+            plane = sb.tile([P, T], U8, name=name, align_bytes=64)
+            nc.vector.memset(plane[:].bitcast(I32), 0)
+            for q in range(QUADS):
+                nc.vector.tensor_copy(out=plane[QUAD * q : QUAD * q + 4, :].bitcast(I32), in_=rows[q].bitcast(I32))
+            return plane
+
         ws_rows = sb.tile([4, QUADS, 2, R], U8, name="ws_rows", align_bytes=64)
-        for i, src in enumerate((w_scales, w0_scales)):
-            nc.sync.dma_start(
-                out=ws_rows[:, :, i, :].bitcast(I32),
-                in_=src[0].rearrange("(q r) c -> r q c", r=4).bitcast(I32),
-            )
+        tb_rows = tb.rearrange("(p t) x -> t p x", t=PACK)
+        tb_t = [sb.tile([P, X], F32, name="tb%d" % t) for t in range(PACK)]
+        load_rows(nc.sync, ws_rows[:, :, 0, :], w_scales)
+        load_rows(nc.sync, ws_rows[:, :, 1, :], w0_scales)
         l1 = load_list("l1", offs)
         xt_s = load_scales(nc.vector, nc.sync, "xt_s", xt_scales)
+        xt_w = load_words(nc.sync, "xt_w", flat(xt_words), T, U32)
         w_w = load_words(nc.sync, "w_w", w_words[0], R, U16)
         w0_w = load_words(nc.sync, "w0_w", flat(w0_words), R, U32)
         l2 = load_list("l2", offs2)
         xo_s = load_scales(nc.vector, nc.sync, "xo_s", xo_scales)
         xo_w = load_words(nc.sync, "xo_w", xo_words[0], T, U16)
-        vs_s = load_scales(nc.gpsimd, nc.gpsimd, "vs_s", vs_scales)
-
-        tb_rows = tb.rearrange("(p t) x -> t p x", t=PACK)
-        tb_t = [sb.tile([P, X], F32, name="tb%d" % t) for t in range(PACK)]
         nc.sync.dma_start(out=tb_t[0][:], in_=tb_rows[0])
         l4 = load_list("l4", offs4)
         l5 = load_list("l5", offs5)
         l3 = load_list("l3", offs3)
+        nc.sync.dma_start(out=tb_t[1][:], in_=tb_rows[1])
+        nc.sync.dma_start(out=tb_t[2][:], in_=tb_rows[2])
         l6 = load_list("l6", offs6)
-        for t in range(1, PACK):
-            nc.sync.dma_start(out=tb_t[t][:], in_=tb_rows[t])
+        vs_s = load_scales(nc.vector, nc.sync, "vs_s", vs_scales)
+        nc.sync.dma_start(out=tb_t[3][:], in_=tb_rows[3])
         vs_w = load_words(nc.sync, "vs_w", flat(vs_words), T, U32)
         l7 = load_list("l7", offs7)
 
         pages = [sb.tile([P, E], F32, name="page%d" % h) for h in range(2)]
-        for page in pages:
-            nc.vector.memset(page[:], 0.0)
+        nc.vector.memset(pages[0][:], 0.0)
+        nc.vector.memset(pages[1][:], 0.0)
 
-        ws_plane = sb.tile([P, 2 * R], U8, name="ws_plane", align_bytes=64)
-        nc.vector.memset(ws_plane[:].bitcast(I32), 0)
-        for q in range(QUADS):
+        ws_plane = spread("ws_plane", [ws_rows[:, q, :, :].rearrange("r i c -> r (i c)") for q in range(QUADS)])
+        ws_d = [sb.tile([P, PACK, P], U8, name="ws_d%d" % i, align_bytes=64) for i in range(2)]
+
+        def deal_scales(i):
             nc.vector.tensor_copy(
-                out=ws_plane[QUAD * q : QUAD * q + 4, :].bitcast(I32),
-                in_=ws_rows[:, q, :, :].rearrange("r i c -> r (i c)").bitcast(I32),
+                out=ws_d[i][:].rearrange("p t m -> p m t"),
+                in_=ws_plane[:, R * i : R * (i + 1)].rearrange("p (m t) -> p m t", t=PACK),
             )
-        ws_d = sb.tile([P, 2, PACK, P], U8, name="ws_d", align_bytes=64)
-        nc.vector.tensor_copy(
-            out=ws_d[:].rearrange("p i t m -> p i m t"),
-            in_=ws_plane[:].rearrange("p (i m t) -> p i m t", i=2, t=PACK),
-        )
+
+        deal_scales(0)
         w_d = sb.tile([P, PACK, P], U16, name="w_d", align_bytes=64)
         w0_d = sb.tile([P, PACK, P], U32, name="w0_d", align_bytes=64)
         for dealt, raw in ((w_d, w_w), (w0_d, w0_w)):
@@ -115,37 +120,57 @@ def tile_list_leadbounds_bank_store_scattered_kernel(
 
         xt_sg = gather("xt_sg", xt_s, l1, J, U8)
         xt_g = gather("xt_g", xt_w, l1, J, U32)
-        xo_sg = gather("xo_sg", xo_s, l2, J, U8)
+        deal_scales(1)
         xo_g = gather("xo_g", xo_w, l2, J, U16)
+        xo_sg = gather("xo_sg", xo_s, l2, J, U8)
 
         acc = [ps.tile([P, J], F32, name="acc%d" % t) for t in range(PACK)]
         for t in range(PACK):
             nc.tensor.matmul_mx(
-                out=acc[t][:], lhsT=w_d[:, t, :].bitcast(E2M1), lhsT_scale=ws_d[:, 0, t, :],
+                out=acc[t][:], lhsT=w_d[:, t, :].bitcast(E2M1), lhsT_scale=ws_d[0][:, t, :],
                 rhs=xt_g[:].bitcast(E4M3), rhs_scale=xt_sg[:], start=True, stop=False,
             )
         for t in range(PACK):
             nc.tensor.matmul_mx(
-                out=acc[t][:], lhsT=w0_d[:, t, :].bitcast(E5M2), lhsT_scale=ws_d[:, 1, t, :],
+                out=acc[t][:], lhsT=w0_d[:, t, :].bitcast(E5M2), lhsT_scale=ws_d[1][:, t, :],
                 rhs=xo_g[:].bitcast(E2M1), rhs_scale=xo_sg[:], start=False, stop=True,
             )
 
-        vs_sg = gather("vs_sg", vs_s, l6, N, U8)
 
         picked = sb.tile([P, PACK, O], F32, name="picked")
         upper = sb.tile([P, PACK, O], F32, name="upper")
         lower = sb.tile([P, PACK, O], F32, name="lower")
         cut = sb.tile([P, PACK, O], F32, name="cut")
-        for t in range(PACK):
-            a_t = sb.tile([P, J], F32, name="a%d" % t)
-            if t < 2:
-                nc.vector.tensor_copy(out=a_t[:], in_=acc[t][:])
+        a_t = [sb.tile([P, J], F32, name="a%d" % t) for t in range(PACK)]
+
+        def leave_psum(t):
+            if t % 2 == 0:
+                nc.vector.tensor_copy(out=a_t[t][:], in_=acc[t][:])
             else:
-                nc.scalar.copy(out=a_t[:], in_=acc[t][:])
-            nc.scalar.activation(out=upper[:, t, :], in_=tb_t[t][:].indirect(l4[:]), func=COPY, scale=a_t[:, 0:1])
-            nc.scalar.activation(out=lower[:, t, :], in_=tb_t[t][:].indirect(l5[:]), func=COPY, scale=a_t[:, 128:129])
-            nc.vector.tensor_copy(out=picked[:, t, :], in_=a_t[:].indirect(l3[:]))
-            nc.vector.tensor_tensor(out=cut[:, t, :], in0=picked[:, t, :], in1=upper[:, t, :], op=MIN)
+                nc.scalar.copy(out=a_t[t][:], in_=acc[t][:])
+
+        def bound(dst, offsets, slot, t):
+            nc.scalar.activation(
+                out=dst[:, t, :], in_=tb_t[t][:].indirect(offsets[:]), func=COPY, scale=a_t[t][:, slot : slot + 1]
+            )
+
+        leave_psum(0)
+        leave_psum(1)
+        leave_psum(2)
+        bound(upper, l4, 0, 0)
+        bound(lower, l5, 128, 0)
+        leave_psum(3)
+        bound(upper, l4, 0, 1)
+        bound(lower, l5, 128, 1)
+        bound(upper, l4, 0, 2)
+        bound(lower, l5, 128, 2)
+        bound(upper, l4, 0, 3)
+        bound(lower, l5, 128, 3)
+        for t in range(PACK):
+            nc.vector.tensor_copy(out=picked[:, t, :], in_=a_t[t][:].indirect(l3[:]))
+        vs_sg = gather("vs_sg", vs_s, l6, N, U8)
+        for ts in (slice(0, 3), slice(3, 4)):
+            nc.vector.tensor_tensor(out=cut[:, ts, :], in0=picked[:, ts, :], in1=upper[:, ts, :], op=MIN)
 
         hid = sb.tile([P, O * PACK], BF16, name="hid", align_bytes=64)
         nc.vector.tensor_tensor(

from contextlib import ExitStack

import concourse.mybir as mybir

F32 = mybir.dt.float32
BF16 = mybir.dt.bfloat16
I32 = mybir.dt.int32
U32 = mybir.dt.uint32
U16 = mybir.dt.uint16
U8 = mybir.dt.uint8
E4M3 = mybir.dt.float8_e4m3fn_x4
E5M2 = mybir.dt.float8_e5m2_x4
E2M1 = mybir.dt.float4_e2m1fn_x4
COPY = mybir.ActivationFunctionType.Copy
MIN = mybir.AluOpType.min
MAX = mybir.AluOpType.max

P = 128
PACK = 4
QUADS = 4
QUAD = 32
T, J, R, X, O, N, E = 1024, 256, 512, 1024, 128, 256, 1024

FLOPS = 2 * 512 * (2 * R * J + N * O)


def tile_list_leadbounds_bank_store_scattered_kernel(
    tc, xt_words, xt_scales, xo_words, xo_scales, w_words, w_scales, w0_words, w0_scales, tb,
    vs_words, vs_scales, offs, offs2, offs3, offs4, offs5, offs6, offs7, out,
):
    nc = tc.nc
    with ExitStack() as ctx:
        lists = ctx.enter_context(tc.tile_pool(name="lists", bufs=1))
        sb = ctx.enter_context(tc.tile_pool(name="sb", bufs=1))
        ps = ctx.enter_context(tc.psum_pool(name="ps", bufs=1))

        def load_list(name, src):
            tile = lists.tile(list(src.shape), U16, name=name)
            nc.sync.dma_start(tile[:], src)
            return tile

        def load_words(queue, name, src, columns, dtype):
            tile = sb.tile([P, columns], dtype, name=name, align_bytes=64)
            queue.dma_start(out=tile[:].bitcast(I32), in_=src.bitcast(I32))
            return tile

        def load_scales(engine, queue, name, src):
            tile = sb.tile([P, T], U8, name=name, align_bytes=64)
            engine.memset(tile[:].bitcast(I32), 0)
            for q in range(QUADS):
                queue.dma_start(
                    out=tile[QUAD * q : QUAD * q + 4, :].bitcast(I32),
                    in_=src[0, 4 * q : 4 * q + 4, :].bitcast(I32),
                )
            return tile

        def gather(name, window, offsets, count, dtype):
            tile = sb.tile([P, count], dtype, name=name, align_bytes=64)
            nc.vector.tensor_copy(out=tile[:], in_=window[:].indirect(offsets[:]))
            return tile

        flat = lambda words: words[0].rearrange("p c t -> p (c t)")

        def load_rows(queue, rows, src):
            queue.dma_start(out=rows.bitcast(I32), in_=src[0].rearrange("(q r) c -> r q c", r=4).bitcast(I32))

        def spread(name, rows):
            plane = sb.tile([P, T], U8, name=name, align_bytes=64)
            nc.vector.memset(plane[:].bitcast(I32), 0)
            for q in range(QUADS):
                nc.vector.tensor_copy(out=plane[QUAD * q : QUAD * q + 4, :].bitcast(I32), in_=rows[q].bitcast(I32))
            return plane

        ws_rows = sb.tile([4, QUADS, 2, R], U8, name="ws_rows", align_bytes=64)
        tb_rows = tb.rearrange("(p t) x -> t p x", t=PACK)
        tb_t = [sb.tile([P, X], F32, name="tb%d" % t) for t in range(PACK)]
        load_rows(nc.sync, ws_rows[:, :, 0, :], w_scales)
        load_rows(nc.sync, ws_rows[:, :, 1, :], w0_scales)
        l1 = load_list("l1", offs)
        xt_s = load_scales(nc.vector, nc.sync, "xt_s", xt_scales)
        xt_w = load_words(nc.sync, "xt_w", flat(xt_words), T, U32)
        w_w = load_words(nc.sync, "w_w", w_words[0], R, U16)
        w0_w = load_words(nc.sync, "w0_w", flat(w0_words), R, U32)
        l2 = load_list("l2", offs2)
        xo_s = load_scales(nc.vector, nc.sync, "xo_s", xo_scales)
        xo_w = load_words(nc.sync, "xo_w", xo_words[0], T, U16)
        nc.sync.dma_start(out=tb_t[0][:], in_=tb_rows[0])
        l4 = load_list("l4", offs4)
        l5 = load_list("l5", offs5)
        l3 = load_list("l3", offs3)
        nc.sync.dma_start(out=tb_t[1][:], in_=tb_rows[1])
        nc.sync.dma_start(out=tb_t[2][:], in_=tb_rows[2])
        l6 = load_list("l6", offs6)
        vs_s = load_scales(nc.vector, nc.sync, "vs_s", vs_scales)
        nc.sync.dma_start(out=tb_t[3][:], in_=tb_rows[3])
        vs_w = load_words(nc.sync, "vs_w", flat(vs_words), T, U32)
        l7 = load_list("l7", offs7)

        pages = [sb.tile([P, E], F32, name="page%d" % h) for h in range(2)]
        nc.vector.memset(pages[0][:], 0.0)
        nc.vector.memset(pages[1][:], 0.0)

        ws_plane = spread("ws_plane", [ws_rows[:, q, :, :].rearrange("r i c -> r (i c)") for q in range(QUADS)])
        ws_d = [sb.tile([P, PACK, P], U8, name="ws_d%d" % i, align_bytes=64) for i in range(2)]

        def deal_scales(i):
            nc.vector.tensor_copy(
                out=ws_d[i][:].rearrange("p t m -> p m t"),
                in_=ws_plane[:, R * i : R * (i + 1)].rearrange("p (m t) -> p m t", t=PACK),
            )

        deal_scales(0)
        w_d = sb.tile([P, PACK, P], U16, name="w_d", align_bytes=64)
        w0_d = sb.tile([P, PACK, P], U32, name="w0_d", align_bytes=64)
        for dealt, raw in ((w_d, w_w), (w0_d, w0_w)):
            nc.scalar.copy(
                out=dealt[:].rearrange("p t m -> p m t"),
                in_=raw[:].rearrange("p (m t) -> p m t", t=PACK),
            )

        xt_sg = gather("xt_sg", xt_s, l1, J, U8)
        xt_g = gather("xt_g", xt_w, l1, J, U32)
        deal_scales(1)
        xo_g = gather("xo_g", xo_w, l2, J, U16)
        xo_sg = gather("xo_sg", xo_s, l2, J, U8)

        acc = [ps.tile([P, J], F32, name="acc%d" % t) for t in range(PACK)]
        for t in range(PACK):
            nc.tensor.matmul_mx(
                out=acc[t][:], lhsT=w_d[:, t, :].bitcast(E2M1), lhsT_scale=ws_d[0][:, t, :],
                rhs=xt_g[:].bitcast(E4M3), rhs_scale=xt_sg[:], start=True, stop=False,
            )
        for t in range(PACK):
            nc.tensor.matmul_mx(
                out=acc[t][:], lhsT=w0_d[:, t, :].bitcast(E5M2), lhsT_scale=ws_d[1][:, t, :],
                rhs=xo_g[:].bitcast(E2M1), rhs_scale=xo_sg[:], start=False, stop=True,
            )


        picked = sb.tile([P, PACK, O], F32, name="picked")
        upper = sb.tile([P, PACK, O], F32, name="upper")
        lower = sb.tile([P, PACK, O], F32, name="lower")
        cut = sb.tile([P, PACK, O], F32, name="cut")
        a_t = [sb.tile([P, J], F32, name="a%d" % t) for t in range(PACK)]

        def leave_psum(t):
            if t % 2 == 0:
                nc.vector.tensor_copy(out=a_t[t][:], in_=acc[t][:])
            else:
                nc.scalar.copy(out=a_t[t][:], in_=acc[t][:])

        def bound(dst, offsets, slot, t):
            nc.scalar.activation(
                out=dst[:, t, :], in_=tb_t[t][:].indirect(offsets[:]), func=COPY, scale=a_t[t][:, slot : slot + 1]
            )

        leave_psum(0)
        leave_psum(1)
        leave_psum(2)
        bound(upper, l4, 0, 0)
        bound(lower, l5, 128, 0)
        leave_psum(3)
        bound(upper, l4, 0, 1)
        bound(lower, l5, 128, 1)
        bound(upper, l4, 0, 2)
        bound(lower, l5, 128, 2)
        bound(upper, l4, 0, 3)
        bound(lower, l5, 128, 3)
        for t in range(PACK):
            nc.vector.tensor_copy(out=picked[:, t, :], in_=a_t[t][:].indirect(l3[:]))
        vs_sg = gather("vs_sg", vs_s, l6, N, U8)
        for ts in (slice(0, 3), slice(3, 4)):
            nc.vector.tensor_tensor(out=cut[:, ts, :], in0=picked[:, ts, :], in1=upper[:, ts, :], op=MIN)

        hid = sb.tile([P, O * PACK], BF16, name="hid", align_bytes=64)
        nc.vector.tensor_tensor(
            out=hid[:].rearrange("p (c i t) -> p c t i", i=4, t=PACK),
            in0=cut[:].rearrange("p t (c i) -> p c t i", i=4),
            in1=lower[:].rearrange("p t (c i) -> p c t i", i=4),
            op=MAX,
        )
        vs_g = gather("vs_g", vs_w, l6, N, U32)
        hid_w = sb.tile([P, O], U32, name="hid_w", align_bytes=64)
        hid_s = sb.tile([P, O], U8, name="hid_s", align_bytes=64)
        nc.vector.quantize_mx(out=hid_w[:].bitcast(E4M3), scales=hid_s[:], in_=hid[:])

        for h in range(2):
            cols = slice(P * h, P * (h + 1))
            prod = ps.tile([P, O], F32, name="prod%d" % h)
            nc.tensor.matmul_mx(
                out=prod[:], lhsT=vs_g[:, cols].bitcast(E5M2), lhsT_scale=vs_sg[:, cols],
                rhs=hid_w[:].bitcast(E4M3), rhs_scale=hid_s[:], start=True, stop=True,
            )
            p_h = sb.tile([P, O], F32, name="p%d" % h)
            if h == 0:
                nc.vector.tensor_copy(out=p_h[:], in_=prod[:])
                nc.vector.tensor_copy(out=pages[h][:].indirect(l7[:]), in_=p_h[:])
                nc.sync.dma_start(out=out[cols, :], in_=pages[h][:])
            else:
                nc.scalar.copy(out=p_h[:], in_=prod[:])
                nc.scalar.activation(out=pages[h][:].indirect(l7[:]), in_=p_h[:], func=COPY)
                nc.scalar.dma_start(out=out[cols, :], in_=pages[h][:])
